import numpy as np
import ml_dtypes


def mxq(x, axis, fmt="e4m3"):
    dtype, down = {"e4m3": (ml_dtypes.float8_e4m3fn, 7), "e5m2": (ml_dtypes.float8_e5m2, 14)}[fmt]
    v = np.moveaxis(np.asarray(x, np.float32).astype(ml_dtypes.bfloat16).astype(np.float64), axis, -1)
    blocks = v.reshape(v.shape[:-1] + (-1, 32))
    amax = np.abs(blocks).max(-1, keepdims=True)
    byte = np.maximum(np.where(amax > 0, np.frexp(amax)[1] - 1 + 127, 0) - down, 1)
    scale = np.exp2(byte - 127.0)
    codes = (blocks / scale).astype(np.float32).astype(dtype).astype(np.float64)
    return np.moveaxis((codes * scale).reshape(v.shape), -1, axis)


WIDE = False


def mx_kscale(k):
    if not WIDE:
        return np.ones(k)
    levels = np.array([10, -10, 5, -5, 0])
    if k % 512:
        return np.exp2(np.random.permutation(np.resize(levels, k // 32))).repeat(32)
    a = np.empty((k // 512, 16))
    for p in range(k // 512):
        a[p, :8] = np.random.permutation(np.resize(levels, 8))
        for g in range(8):
            far = levels[np.abs(levels - a[p, g]) >= 10]
            a[p, g + 8] = far[np.random.randint(len(far))]
    return np.exp2(a.ravel()).repeat(32)


def f64(x):
    return np.asarray(x).astype(np.float64)


def striped(idx):
    return np.tile(idx.reshape(-1, 16).T, (8, 1)).astype(np.uint16)


def unstriped(offs):
    return offs[:16].T.reshape(-1).astype(np.int64)


def pack_weight(w):
    k, n = w.shape
    w = f64(np.asarray(w, np.float32).astype(ml_dtypes.bfloat16)).reshape(k // 32, 32, n)
    amax = np.abs(w).max(1)
    byte = np.clip(np.where(amax > 0, np.frexp(amax)[1] - 1 + 127 - 7, 1), 1, 254)
    scaled = (w * np.exp2(127.0 - byte)[:, None, :]).reshape(k, n).astype(np.float32)
    words = np.ascontiguousarray(scaled.reshape(k // 512, 128, 4, n).transpose(0, 1, 3, 2)).astype(ml_dtypes.float8_e4m3fn).view(np.uint8)
    return words, np.ascontiguousarray(byte.astype(np.uint8).reshape(k // 512, 16, n))


def unpack_weight(words, scales):
    g, p, n, _ = words.shape
    vals = np.ascontiguousarray(words).view(ml_dtypes.float8_e4m3fn).astype(np.float64) * np.repeat(np.exp2(scales.astype(np.float64) - 127.0), 8, axis=1)[..., None]
    return vals.transpose(0, 1, 3, 2).reshape(g * 512, n)


K, T, S, J = 512, 1024, 512, 512
P = 2 ** 7


def setup_inputs():
    n = np.random.standard_normal
    s = mx_kscale(K)[:, None]
    packed_xT = pack_weight(n((K, T)) * s)
    return {
        "x_words": packed_xT[0],
        "x_scales": packed_xT[1],
        "hT": (n((K, J)) / np.sqrt(K) / s).astype(np.float32),
        "corr": (np.tile(0.5 * np.random.standard_normal(T), (P, 1))).astype(np.float32),
        "offs": striped(np.random.permutation(T)[:S]),
    }


def reference(x_words, x_scales, hT, corr, offs):
    hTq = mxq(f64(hT), 0, "e4m3")
    xq = unpack_weight(x_words, x_scales)[:, unstriped(offs)]
    y = (hTq.T @ xq) + f64(corr)[:1][:, unstriped(offs)]
    l = 2.0 * np.tanh(0.5 * y)
    e = np.exp(l - l.max(axis=1, keepdims=True))
    return e / e.sum(axis=1, keepdims=True)

@@ -1,0 +1,165 @@
+from contextlib import ExitStack
+
+import concourse.mybir as mybir
+from concourse.masks import make_identity
+
+K, T, S, J = 512, 1024, 512, 512
+FLOPS = 2 * K * S * J
+
+F32 = mybir.dt.float32
+BF16 = mybir.dt.bfloat16
+I32 = mybir.dt.int32
+U32 = mybir.dt.uint32
+U16 = mybir.dt.uint16
+U8 = mybir.dt.uint8
+FP8X4 = mybir.dt.float8_e4m3fn_x4
+ACT = mybir.ActivationFunctionType
+ALU = mybir.AluOpType
+
+P = 128
+PACK = 4
+HALF = 256
+CORR_ROW = P - 1
+CAP = 2.0
+
+
+def tile_picked_zsoft_cap_p_kernel(tc, x_words, x_scales, hT, corr, offs, out):
+    nc = tc.nc
+    with ExitStack() as ctx:
+        keep = ctx.enter_context(tc.tile_pool(name="keep", bufs=1))
+        score_banks = ctx.enter_context(tc.psum_pool(name="score_banks", bufs=4))
+        row_banks = ctx.enter_context(tc.psum_pool(name="row_banks", bufs=4))
+
+        offsets = keep.tile([P, S // 16], U16, name="offsets")
+        nc.sync.dma_start(offsets[:], offs)
+
+        corr_table = keep.tile([P, T], F32, name="corr_table")
+        nc.sync.dma_start(corr_table[CORR_ROW:P, :], corr[CORR_ROW:P, :])
+
+        scale_table = keep.tile([P, T], U8, name="scale_table", align_bytes=64)
+        scale_rows = x_scales[0].bitcast(I32)
+        for q in range(4):
+            nc.sync.dma_start(
+                scale_table[32 * q : 32 * (q + 1), :].bitcast(I32),
+                scale_rows[4 * q : 4 * (q + 1), :].partition_broadcast(8),
+            )
+
+        h_rows = hT.rearrange("(p r) t -> p r t", r=PACK)
+        h_first = keep.tile([P, PACK, HALF], F32, name="h_first", tag="first", align_bytes=64)
+        nc.sync.dma_start(h_first[:], h_rows[:, :, 0:HALF])
+
+        word_table = keep.tile([P, T], I32, name="word_table", align_bytes=64)
+        nc.sync.dma_start(word_table[:], x_words[0].rearrange("p c r -> p (c r)").bitcast(I32))
+
+        h_second = keep.tile([P, 2, PACK, P], F32, name="h_second", tag="late")
+        for v in range(2):
+            nc.sync.dma_start(h_second[:, v], h_rows[:, :, HALF + P * v : HALF + P * (v + 1)])
+
+        shift = keep.tile([P, 1], F32, name="shift")
+        nc.vector.memset(shift[:], -CAP)
+        nc.vector.memset(corr_table[0:CORR_ROW, :], 0.0)
+        warm = keep.tile([P, 1], F32, name="warm")
+        nc.scalar.activation(warm[:], shift[:], ACT.Exp)
+
+        identity = keep.tile([P, P], F32, name="identity")
+        make_identity(nc, identity[:])
+
+        x_codes = {}
+        x_plane = keep.tile([P, S], U8, name="x_plane", align_bytes=64)
+        corr_picked = keep.tile([P, S], F32, name="corr_picked")
+        h_bf = {
+            lo: keep.tile([P, hi - lo, PACK], BF16, name="h_bf%d" % lo, align_bytes=64)
+            for lo, hi in ((0, HALF), (HALF, HALF + P), (HALF + P, J))
+        }
+        h_codes = {}
+        h_plane = [keep.tile([P, HALF], U8, name="h_plane%d" % u, align_bytes=64) for u in range(2)]
+        half_corr = keep.tile([P, 4], F32, name="half_corr")
+
+        def interleave(lo, raw):
+            nc.scalar.copy(
+                h_bf[lo][:].rearrange("p (c i) r -> p c r i", i=4),
+                raw.rearrange("p r (c i) -> p c r i", i=4),
+            )
+
+        def quantize(lo, hi):
+            nc.vector.quantize_mx(
+                out=h_codes[lo // HALF][:, lo % HALF : lo % HALF + hi - lo].bitcast(FP8X4),
+                scales=h_plane[lo // HALF][:, lo % HALF : lo % HALF + hi - lo],
+                in_=h_bf[lo][:].rearrange("p t r -> p (t r)"),
+            )
+
+        def gather_words(b):
+            nc.vector.tensor_copy(
+                x_codes[b], word_table[:].bitcast(U32).indirect(offsets[:, 8 * b : 8 * (b + 1)])
+            )
+
+        nc.vector.tensor_copy(corr_picked[:], corr_table[:].indirect(offsets[:]))
+        nc.vector.tensor_copy(x_plane[:], scale_table[:].indirect(offsets[:]))
+        corr_bank = row_banks.tile([P, 4, P], F32, name="corr_bank", tag="rows")
+        for b in range(4):
+            nc.tensor.transpose(corr_bank[:, b, :], corr_picked[:, P * b : P * (b + 1)], identity[:])
+        interleave(0, h_first[:])
+        nc.scalar.mul(half_corr[:], corr_bank[:, :, CORR_ROW], 0.5)
+        first_codes = keep.tile([P, P], U32, name="first_codes", align_bytes=64)
+        x_codes[0] = first_codes[:]
+        gather_words(0)
+        h_codes[0] = keep.tile([P, HALF], U32, name="h_codes0", align_bytes=64)
+        quantize(0, HALF)
+        later_codes = keep.tile([P, 3 * P], U32, name="later_codes", tag="first", align_bytes=64)
+        for b in range(1, 4):
+            x_codes[b] = later_codes[:, P * (b - 1) : P * b]
+        for b in range(1, 4):
+            gather_words(b)
+        for v in range(2):
+            interleave(HALF + P * v, h_second[:, v])
+        h_codes[1] = keep.tile([P, HALF], U32, name="h_codes1", tag="second", align_bytes=64)
+        for v in range(2):
+            quantize(HALF + P * v, HALF + P * (v + 1))
+
+        capped = {}
+
+        banks = {}
+
+        def score(u, b):
+            bank = banks[u, b] = score_banks.tile([P, HALF], F32, name="score", tag="score")
+            nc.tensor.matmul_mx(
+                out=bank[:],
+                lhsT=x_codes[b].bitcast(FP8X4),
+                lhsT_scale=x_plane[:, P * b : P * (b + 1)],
+                rhs=h_codes[u][:].bitcast(FP8X4),
+                rhs_scale=h_plane[u][:],
+                start=True,
+                stop=True,
+            )
+            capped[u, b] = keep.tile([P, HALF], F32, name="capped%d_%d" % (u, b), tag="late" if (u, b) == (0, 0) else "capped%d_%d" % (u, b))
+
+        def cap(u, b, lo, hi):
+            nc.scalar.activation(
+                capped[u, b][:, lo:hi], banks[u, b][:, lo:hi], ACT.Tanh, bias=half_corr[:, b : b + 1], scale=0.5
+            )
+
+        def softmax(tb):
+            u, v = divmod(tb, 2)
+            bank = row_banks.tile([P, S], F32, name="rows", tag="rows")
+            for b in range(4):
+                nc.tensor.transpose(bank[:, P * b : P * (b + 1)], capped[u, b][:, P * v : P * (v + 1)], identity[:])
+            weights = keep.tile([P, S], F32, name="weights%d" % tb, tag="second" if tb == 1 else "weights%d" % tb, align_bytes=64)
+            total = keep.tile([P, 1], F32, name="total%d" % tb)
+            inverse = keep.tile([P, 1], F32, name="inverse%d" % tb)
+            result = keep.tile([P, S], F32, name="result%d" % tb)
+            nc.scalar.activation(weights[:], bank[:], ACT.Exp, bias=shift[:], scale=CAP, accum_out=total[:])
+            nc.vector.reciprocal(inverse[:], total[:])
+            nc.vector.tensor_scalar(result[:], weights[:], inverse[:], None, ALU.mult)
+            nc.sync.dma_start(out[P * tb : P * (tb + 1), :], result[:])
+
+        for b in range(4):
+            score(0, b)
+            cap(0, b, 0, HALF)
+        for b in range(4):
+            score(1, b)
+            cap(1, b, 0, HALF)
+            if b == 1:
+                softmax(0)
+        softmax(1)
+        softmax(2)
+        softmax(3)

@@ -27,8 +27,8 @@ def tile_picked_zsoft_cap_p_kernel(tc, x_words, x_scales, hT, corr, offs, out):
     nc = tc.nc
     with ExitStack() as ctx:
         keep = ctx.enter_context(tc.tile_pool(name="keep", bufs=1))
-        score_banks = ctx.enter_context(tc.psum_pool(name="score_banks", bufs=4))
-        row_banks = ctx.enter_context(tc.psum_pool(name="row_banks", bufs=4))
+        score_banks = ctx.enter_context(tc.psum_pool(name="score_banks", bufs=5))
+        row_banks = ctx.enter_context(tc.psum_pool(name="row_banks", bufs=3))
 
         offsets = keep.tile([P, S // 16], U16, name="offsets")
         nc.sync.dma_start(offsets[:], offs)
@@ -38,22 +38,17 @@ def tile_picked_zsoft_cap_p_kernel(tc, x_words, x_scales, hT, corr, offs, out):
 
         scale_table = keep.tile([P, T], U8, name="scale_table", align_bytes=64)
         scale_rows = x_scales[0].bitcast(I32)
+        nc.vector.memset(scale_table[:].bitcast(I32), 0)
         for q in range(4):
-            nc.sync.dma_start(
-                scale_table[32 * q : 32 * (q + 1), :].bitcast(I32),
-                scale_rows[4 * q : 4 * (q + 1), :].partition_broadcast(8),
-            )
-
-        h_rows = hT.rearrange("(p r) t -> p r t", r=PACK)
-        h_first = keep.tile([P, PACK, HALF], F32, name="h_first", tag="first", align_bytes=64)
-        nc.sync.dma_start(h_first[:], h_rows[:, :, 0:HALF])
+            nc.sync.dma_start(scale_table[32 * q : 32 * q + 4, :].bitcast(I32), scale_rows[4 * q : 4 * (q + 1), :])
 
         word_table = keep.tile([P, T], I32, name="word_table", align_bytes=64)
         nc.sync.dma_start(word_table[:], x_words[0].rearrange("p c r -> p (c r)").bitcast(I32))
 
-        h_second = keep.tile([P, 2, PACK, P], F32, name="h_second", tag="late")
-        for v in range(2):
-            nc.sync.dma_start(h_second[:, v], h_rows[:, :, HALF + P * v : HALF + P * (v + 1)])
+        h_rows = hT.rearrange("(p r) t -> p r t", r=PACK)
+        h_raw = [keep.tile([P, PACK, P], F32, name="h_raw%d" % tb, tag="h_raw%d" % tb, align_bytes=64) for tb in range(4)]
+        for tb in range(4):
+            nc.sync.dma_start(h_raw[tb][:], h_rows[:, :, P * tb : P * (tb + 1)])
 
         shift = keep.tile([P, 1], F32, name="shift")
         nc.vector.memset(shift[:], -CAP)
@@ -67,83 +62,67 @@ def tile_picked_zsoft_cap_p_kernel(tc, x_words, x_scales, hT, corr, offs, out):
         x_codes = {}
         x_plane = keep.tile([P, S], U8, name="x_plane", align_bytes=64)
         corr_picked = keep.tile([P, S], F32, name="corr_picked")
-        h_bf = {
-            lo: keep.tile([P, hi - lo, PACK], BF16, name="h_bf%d" % lo, align_bytes=64)
-            for lo, hi in ((0, HALF), (HALF, HALF + P), (HALF + P, J))
-        }
-        h_codes = {}
+        h_bf = [keep.tile([P, P, PACK], BF16, name="h_bf%d" % tb, align_bytes=64) for tb in range(4)]
+        h_codes = [keep.tile([P, HALF], U32, name="h_codes%d" % u, tag="h_codes%d" % u, align_bytes=64) for u in range(2)]
         h_plane = [keep.tile([P, HALF], U8, name="h_plane%d" % u, align_bytes=64) for u in range(2)]
-        half_corr = keep.tile([P, 4], F32, name="half_corr")
 
-        def interleave(lo, raw):
+        def quantize(tb):
+            u, v = divmod(tb, 2)
             nc.scalar.copy(
-                h_bf[lo][:].rearrange("p (c i) r -> p c r i", i=4),
-                raw.rearrange("p r (c i) -> p c r i", i=4),
+                h_bf[tb][:].rearrange("p (c i) r -> p c r i", i=4),
+                h_raw[tb][:].rearrange("p r (c i) -> p c r i", i=4),
             )
-
-        def quantize(lo, hi):
             nc.vector.quantize_mx(
-                out=h_codes[lo // HALF][:, lo % HALF : lo % HALF + hi - lo].bitcast(FP8X4),
-                scales=h_plane[lo // HALF][:, lo % HALF : lo % HALF + hi - lo],
-                in_=h_bf[lo][:].rearrange("p t r -> p (t r)"),
+                out=h_codes[u][:, P * v : P * (v + 1)].bitcast(FP8X4),
+                scales=h_plane[u][:, P * v : P * (v + 1)],
+                in_=h_bf[tb][:].rearrange("p t r -> p (t r)"),
             )
 
-        def gather_words(b):
-            nc.vector.tensor_copy(
-                x_codes[b], word_table[:].bitcast(U32).indirect(offsets[:, 8 * b : 8 * (b + 1)])
-            )
+        def gather_words(blocks, tag):
+            picked = keep.tile([P, P * len(blocks)], U32, name="x_codes%d" % blocks[0], tag=tag, align_bytes=64)
+            for i, b in enumerate(blocks):
+                x_codes[b] = picked[:, P * i : P * (i + 1)]
+                nc.vector.tensor_copy(x_codes[b], word_table[:].bitcast(U32).indirect(offsets[:, 8 * b : 8 * (b + 1)]))
 
         nc.vector.tensor_copy(corr_picked[:], corr_table[:].indirect(offsets[:]))
         nc.vector.tensor_copy(x_plane[:], scale_table[:].indirect(offsets[:]))
         corr_bank = row_banks.tile([P, 4, P], F32, name="corr_bank", tag="rows")
         for b in range(4):
             nc.tensor.transpose(corr_bank[:, b, :], corr_picked[:, P * b : P * (b + 1)], identity[:])
-        interleave(0, h_first[:])
+        gather_words([0, 1], "x_codes0")
+        quantize(0)
+        quantize(1)
+        half_corr = keep.tile([P, 4], F32, name="half_corr", tag="h_raw0", align_bytes=64)
         nc.scalar.mul(half_corr[:], corr_bank[:, :, CORR_ROW], 0.5)
-        first_codes = keep.tile([P, P], U32, name="first_codes", align_bytes=64)
-        x_codes[0] = first_codes[:]
-        gather_words(0)
-        h_codes[0] = keep.tile([P, HALF], U32, name="h_codes0", align_bytes=64)
-        quantize(0, HALF)
-        later_codes = keep.tile([P, 3 * P], U32, name="later_codes", tag="first", align_bytes=64)
-        for b in range(1, 4):
-            x_codes[b] = later_codes[:, P * (b - 1) : P * b]
-        for b in range(1, 4):
-            gather_words(b)
-        for v in range(2):
-            interleave(HALF + P * v, h_second[:, v])
-        h_codes[1] = keep.tile([P, HALF], U32, name="h_codes1", tag="second", align_bytes=64)
-        for v in range(2):
-            quantize(HALF + P * v, HALF + P * (v + 1))
+        gather_words([2, 3], "h_raw1")
+        quantize(2)
+        quantize(3)
 
         capped = {}
 
-        banks = {}
-
-        def score(u, b):
-            bank = banks[u, b] = score_banks.tile([P, HALF], F32, name="score", tag="score")
+        def score(b, lo, hi, tag):
+            u = lo // HALF
+            cols = slice(lo % HALF, lo % HALF + hi - lo)
+            bank = score_banks.tile([P, hi - lo], F32, name="score", tag="score")
             nc.tensor.matmul_mx(
                 out=bank[:],
                 lhsT=x_codes[b].bitcast(FP8X4),
                 lhsT_scale=x_plane[:, P * b : P * (b + 1)],
-                rhs=h_codes[u][:].bitcast(FP8X4),
-                rhs_scale=h_plane[u][:],
+                rhs=h_codes[u][:, cols].bitcast(FP8X4),
+                rhs_scale=h_plane[u][:, cols],
                 start=True,
                 stop=True,
             )
-            capped[u, b] = keep.tile([P, HALF], F32, name="capped%d_%d" % (u, b), tag="late" if (u, b) == (0, 0) else "capped%d_%d" % (u, b))
+            piece = keep.tile([P, hi - lo], F32, name="capped", tag=tag, align_bytes=64)
+            nc.scalar.activation(piece[:], bank[:], ACT.Tanh, bias=half_corr[:, b : b + 1], scale=0.5)
+            for t0 in range(lo, hi, P):
+                capped[t0 // P, b] = piece[:, t0 - lo : t0 - lo + P]
 
-        def cap(u, b, lo, hi):
-            nc.scalar.activation(
-                capped[u, b][:, lo:hi], banks[u, b][:, lo:hi], ACT.Tanh, bias=half_corr[:, b : b + 1], scale=0.5
-            )
-
-        def softmax(tb):
-            u, v = divmod(tb, 2)
+        def softmax(tb, tag):
             bank = row_banks.tile([P, S], F32, name="rows", tag="rows")
             for b in range(4):
-                nc.tensor.transpose(bank[:, P * b : P * (b + 1)], capped[u, b][:, P * v : P * (v + 1)], identity[:])
-            weights = keep.tile([P, S], F32, name="weights%d" % tb, tag="second" if tb == 1 else "weights%d" % tb, align_bytes=64)
+                nc.tensor.transpose(bank[:, P * b : P * (b + 1)], capped[tb, b], identity[:])
+            weights = keep.tile([P, S], F32, name="weights", tag=tag, align_bytes=64)
             total = keep.tile([P, 1], F32, name="total%d" % tb)
             inverse = keep.tile([P, 1], F32, name="inverse%d" % tb)
             result = keep.tile([P, S], F32, name="result%d" % tb)
@@ -152,14 +131,15 @@ def tile_picked_zsoft_cap_p_kernel(tc, x_words, x_scales, hT, corr, offs, out):
             nc.vector.tensor_scalar(result[:], weights[:], inverse[:], None, ALU.mult)
             nc.sync.dma_start(out[P * tb : P * (tb + 1), :], result[:])
 
-        for b in range(4):
-            score(0, b)
-            cap(0, b, 0, HALF)
-        for b in range(4):
-            score(1, b)
-            cap(1, b, 0, HALF)
-            if b == 1:
-                softmax(0)
-        softmax(1)
-        softmax(2)
-        softmax(3)
+        score(0, 0, P, "h_raw3")
+        score(0, P, HALF, "capped_second")
+        for b in range(1, 4):
+            score(b, 0, HALF, "capped0_%d" % b)
+        score(0, HALF, J, "capped1_0")
+        score(1, HALF, J, "capped1_1")
+        softmax(0, "weights0")
+        score(2, HALF, J, "capped1_2")
+        score(3, HALF, J, "capped1_3")
+        softmax(1, "h_codes1")
+        softmax(2, "weights2")
+        softmax(3, "weights3")

@@ -27,8 +27,7 @@ def tile_picked_zsoft_cap_p_kernel(tc, x_words, x_scales, hT, corr, offs, out):
     nc = tc.nc
     with ExitStack() as ctx:
         keep = ctx.enter_context(tc.tile_pool(name="keep", bufs=1))
-        score_banks = ctx.enter_context(tc.psum_pool(name="score_banks", bufs=5))
-        row_banks = ctx.enter_context(tc.psum_pool(name="row_banks", bufs=3))
+        psum = ctx.enter_context(tc.psum_pool(name="psum", bufs=1))
 
         offsets = keep.tile([P, S // 16], U16, name="offsets")
         nc.sync.dma_start(offsets[:], offs)
@@ -38,17 +37,21 @@ def tile_picked_zsoft_cap_p_kernel(tc, x_words, x_scales, hT, corr, offs, out):
 
         scale_table = keep.tile([P, T], U8, name="scale_table", align_bytes=64)
         scale_rows = x_scales[0].bitcast(I32)
-        nc.vector.memset(scale_table[:].bitcast(I32), 0)
         for q in range(4):
-            nc.sync.dma_start(scale_table[32 * q : 32 * q + 4, :].bitcast(I32), scale_rows[4 * q : 4 * (q + 1), :])
+            nc.sync.dma_start(
+                scale_table[32 * q : 32 * (q + 1), :].bitcast(I32),
+                scale_rows[4 * q : 4 * (q + 1), :].partition_broadcast(8),
+            )
+
+        h_rows = hT.rearrange("(p r) t -> p r t", r=PACK)
+        h_early = keep.tile([P, PACK, J - P], F32, name="h_early")
+        nc.sync.dma_start(h_early[:], h_rows[:, :, 0 : J - P])
 
         word_table = keep.tile([P, T], I32, name="word_table", align_bytes=64)
         nc.sync.dma_start(word_table[:], x_words[0].rearrange("p c r -> p (c r)").bitcast(I32))
 
-        h_rows = hT.rearrange("(p r) t -> p r t", r=PACK)
-        h_raw = [keep.tile([P, PACK, P], F32, name="h_raw%d" % tb, tag="h_raw%d" % tb, align_bytes=64) for tb in range(4)]
-        for tb in range(4):
-            nc.sync.dma_start(h_raw[tb][:], h_rows[:, :, P * tb : P * (tb + 1)])
+        h_late = keep.tile([P, PACK, P], F32, name="h_late", tag="h_late")
+        nc.sync.dma_start(h_late[:], h_rows[:, :, J - P : J])
 
         shift = keep.tile([P, 1], F32, name="shift")
         nc.vector.memset(shift[:], -CAP)
@@ -59,70 +62,68 @@ def tile_picked_zsoft_cap_p_kernel(tc, x_words, x_scales, hT, corr, offs, out):
         identity = keep.tile([P, P], F32, name="identity")
         make_identity(nc, identity[:])
 
-        x_codes = {}
+        x_codes = keep.tile([P, S], U32, name="x_codes", align_bytes=64)
         x_plane = keep.tile([P, S], U8, name="x_plane", align_bytes=64)
         corr_picked = keep.tile([P, S], F32, name="corr_picked")
-        h_bf = [keep.tile([P, P, PACK], BF16, name="h_bf%d" % tb, align_bytes=64) for tb in range(4)]
-        h_codes = [keep.tile([P, HALF], U32, name="h_codes%d" % u, tag="h_codes%d" % u, align_bytes=64) for u in range(2)]
+        h_bf = [keep.tile([P, HALF, PACK], BF16, name="h_bf%d" % u, align_bytes=64) for u in range(2)]
+        h_codes = [keep.tile([P, HALF], U32, name="h_codes%d" % u, align_bytes=64) for u in range(2)]
         h_plane = [keep.tile([P, HALF], U8, name="h_plane%d" % u, align_bytes=64) for u in range(2)]
+        half_corr = keep.tile([P, 4], F32, name="half_corr")
 
-        def quantize(tb):
+        def interleave(copy, tb, raw):
             u, v = divmod(tb, 2)
-            nc.scalar.copy(
-                h_bf[tb][:].rearrange("p (c i) r -> p c r i", i=4),
-                h_raw[tb][:].rearrange("p r (c i) -> p c r i", i=4),
-            )
-            nc.vector.quantize_mx(
-                out=h_codes[u][:, P * v : P * (v + 1)].bitcast(FP8X4),
-                scales=h_plane[u][:, P * v : P * (v + 1)],
-                in_=h_bf[tb][:].rearrange("p t r -> p (t r)"),
+            copy(
+                h_bf[u][:, P * v : P * (v + 1), :].rearrange("p (c i) r -> p c r i", i=4),
+                raw.rearrange("p r (c i) -> p c r i", i=4),
             )
 
-        def gather_words(blocks, tag):
-            picked = keep.tile([P, P * len(blocks)], U32, name="x_codes%d" % blocks[0], tag=tag, align_bytes=64)
-            for i, b in enumerate(blocks):
-                x_codes[b] = picked[:, P * i : P * (i + 1)]
-                nc.vector.tensor_copy(x_codes[b], word_table[:].bitcast(U32).indirect(offsets[:, 8 * b : 8 * (b + 1)]))
+        def quantize(u):
+            nc.vector.quantize_mx(
+                out=h_codes[u][:].bitcast(FP8X4),
+                scales=h_plane[u][:],
+                in_=h_bf[u][:].rearrange("p t r -> p (t r)"),
+            )
 
         nc.vector.tensor_copy(corr_picked[:], corr_table[:].indirect(offsets[:]))
         nc.vector.tensor_copy(x_plane[:], scale_table[:].indirect(offsets[:]))
-        corr_bank = row_banks.tile([P, 4, P], F32, name="corr_bank", tag="rows")
+        corr_bank = psum.tile([P, 4, P], F32, name="corr_bank", tag="bank7")
         for b in range(4):
             nc.tensor.transpose(corr_bank[:, b, :], corr_picked[:, P * b : P * (b + 1)], identity[:])
-        gather_words([0, 1], "x_codes0")
-        quantize(0)
-        quantize(1)
-        half_corr = keep.tile([P, 4], F32, name="half_corr", tag="h_raw0", align_bytes=64)
         nc.scalar.mul(half_corr[:], corr_bank[:, :, CORR_ROW], 0.5)
-        gather_words([2, 3], "h_raw1")
-        quantize(2)
-        quantize(3)
+        interleave(nc.scalar.copy, 0, h_early[:, :, 0:P])
+        interleave(nc.vector.tensor_copy, 1, h_early[:, :, P : 2 * P])
+        interleave(nc.scalar.copy, 2, h_early[:, :, 2 * P : 3 * P])
+        interleave(nc.scalar.copy, 3, h_late[:])
+        quantize(0)
+        for b in range(4):
+            nc.vector.tensor_copy(
+                x_codes[:, P * b : P * (b + 1)], word_table[:].bitcast(U32).indirect(offsets[:, 8 * b : 8 * (b + 1)])
+            )
+        quantize(1)
 
         capped = {}
-
-        def score(b, lo, hi, tag):
-            u = lo // HALF
-            cols = slice(lo % HALF, lo % HALF + hi - lo)
-            bank = score_banks.tile([P, hi - lo], F32, name="score", tag="score")
-            nc.tensor.matmul_mx(
-                out=bank[:],
-                lhsT=x_codes[b].bitcast(FP8X4),
-                lhsT_scale=x_plane[:, P * b : P * (b + 1)],
-                rhs=h_codes[u][:, cols].bitcast(FP8X4),
-                rhs_scale=h_plane[u][:, cols],
-                start=True,
-                stop=True,
-            )
-            piece = keep.tile([P, hi - lo], F32, name="capped", tag=tag, align_bytes=64)
-            nc.scalar.activation(piece[:], bank[:], ACT.Tanh, bias=half_corr[:, b : b + 1], scale=0.5)
-            for t0 in range(lo, hi, P):
-                capped[t0 // P, b] = piece[:, t0 - lo : t0 - lo + P]
-
-        def softmax(tb, tag):
-            bank = row_banks.tile([P, S], F32, name="rows", tag="rows")
+        for u in range(2):
             for b in range(4):
-                nc.tensor.transpose(bank[:, P * b : P * (b + 1)], capped[tb, b], identity[:])
-            weights = keep.tile([P, S], F32, name="weights", tag=tag, align_bytes=64)
+                bank = psum.tile([P, HALF], F32, name="score", tag="bank%d" % (4 * u + b))
+                nc.tensor.matmul_mx(
+                    out=bank[:],
+                    lhsT=x_codes[:, P * b : P * (b + 1)].bitcast(FP8X4),
+                    lhsT_scale=x_plane[:, P * b : P * (b + 1)],
+                    rhs=h_codes[u][:].bitcast(FP8X4),
+                    rhs_scale=h_plane[u][:],
+                    start=True,
+                    stop=True,
+                )
+                tag = "h_late" if (u, b) == (0, 0) else "capped%d_%d" % (u, b)
+                capped[u, b] = keep.tile([P, HALF], F32, name="capped", tag=tag)
+                nc.scalar.activation(capped[u, b][:], bank[:], ACT.Tanh, bias=half_corr[:, b : b + 1], scale=0.5)
+
+        for tb in range(4):
+            u, v = divmod(tb, 2)
+            bank = psum.tile([P, S], F32, name="rows", tag="bank%d" % (3 + tb))
+            for b in range(4):
+                nc.tensor.transpose(bank[:, P * b : P * (b + 1)], capped[u, b][:, P * v : P * (v + 1)], identity[:])
+            weights = keep.tile([P, S], F32, name="weights%d" % tb)
             total = keep.tile([P, 1], F32, name="total%d" % tb)
             inverse = keep.tile([P, 1], F32, name="inverse%d" % tb)
             result = keep.tile([P, S], F32, name="result%d" % tb)
@@ -130,16 +131,3 @@ def tile_picked_zsoft_cap_p_kernel(tc, x_words, x_scales, hT, corr, offs, out):
             nc.vector.reciprocal(inverse[:], total[:])
             nc.vector.tensor_scalar(result[:], weights[:], inverse[:], None, ALU.mult)
             nc.sync.dma_start(out[P * tb : P * (tb + 1), :], result[:])
-
-        score(0, 0, P, "h_raw3")
-        score(0, P, HALF, "capped_second")
-        for b in range(1, 4):
-            score(b, 0, HALF, "capped0_%d" % b)
-        score(0, HALF, J, "capped1_0")
-        score(1, HALF, J, "capped1_1")
-        softmax(0, "weights0")
-        score(2, HALF, J, "capped1_2")
-        score(3, HALF, J, "capped1_3")
-        softmax(1, "h_codes1")
-        softmax(2, "weights2")
-        softmax(3, "weights3")

@@ -65,10 +65,9 @@ def tile_picked_zsoft_cap_p_kernel(tc, x_words, x_scales, hT, corr, offs, out):
         x_codes = keep.tile([P, S], U32, name="x_codes", align_bytes=64)
         x_plane = keep.tile([P, S], U8, name="x_plane", align_bytes=64)
         corr_picked = keep.tile([P, S], F32, name="corr_picked")
-        h_bf = [keep.tile([P, HALF, PACK], BF16, name="h_bf%d" % u, align_bytes=64) for u in range(2)]
+        h_bf = [keep.tile([P, HALF, PACK], BF16, name="h_bf%d" % u, tag="h_bf%d" % u, align_bytes=64) for u in range(2)]
         h_codes = [keep.tile([P, HALF], U32, name="h_codes%d" % u, align_bytes=64) for u in range(2)]
         h_plane = [keep.tile([P, HALF], U8, name="h_plane%d" % u, align_bytes=64) for u in range(2)]
-        half_corr = keep.tile([P, 4], F32, name="half_corr")
 
         def interleave(copy, tb, raw):
             u, v = divmod(tb, 2)
@@ -89,12 +88,13 @@ def tile_picked_zsoft_cap_p_kernel(tc, x_words, x_scales, hT, corr, offs, out):
         corr_bank = psum.tile([P, 4, P], F32, name="corr_bank", tag="bank7")
         for b in range(4):
             nc.tensor.transpose(corr_bank[:, b, :], corr_picked[:, P * b : P * (b + 1)], identity[:])
-        nc.scalar.mul(half_corr[:], corr_bank[:, :, CORR_ROW], 0.5)
         interleave(nc.scalar.copy, 0, h_early[:, :, 0:P])
         interleave(nc.vector.tensor_copy, 1, h_early[:, :, P : 2 * P])
         interleave(nc.scalar.copy, 2, h_early[:, :, 2 * P : 3 * P])
-        interleave(nc.scalar.copy, 3, h_late[:])
         quantize(0)
+        half_corr = keep.tile([P, 4], F32, name="half_corr", tag="h_bf0", align_bytes=64)
+        nc.scalar.mul(half_corr[:], corr_bank[:, :, CORR_ROW], 0.5)
+        interleave(nc.scalar.copy, 3, h_late[:])
         for b in range(4):
             nc.vector.tensor_copy(
                 x_codes[:, P * b : P * (b + 1)], word_table[:].bitcast(U32).indirect(offsets[:, 8 * b : 8 * (b + 1)])

@@ -1,7 +1,6 @@
 from contextlib import ExitStack
 
 import concourse.mybir as mybir
-from concourse.masks import make_identity
 
 K, T, S, J = 512, 1024, 512, 512
 FLOPS = 2 * K * S * J
@@ -32,26 +31,26 @@ def tile_picked_zsoft_cap_p_kernel(tc, x_words, x_scales, hT, corr, offs, out):
         offsets = keep.tile([P, S // 16], U16, name="offsets")
         nc.sync.dma_start(offsets[:], offs)
 
-        corr_table = keep.tile([P, T], F32, name="corr_table")
+        corr_table = keep.tile([P, T], F32, name="corr_table", tag="corr_table", align_bytes=64)
         nc.sync.dma_start(corr_table[CORR_ROW:P, :], corr[CORR_ROW:P, :])
 
         scale_table = keep.tile([P, T], U8, name="scale_table", align_bytes=64)
         scale_rows = x_scales[0].bitcast(I32)
         for q in range(4):
-            nc.sync.dma_start(
+            queue = nc.sync if q == 0 else nc.scalar
+            queue.dma_start(
                 scale_table[32 * q : 32 * (q + 1), :].bitcast(I32),
                 scale_rows[4 * q : 4 * (q + 1), :].partition_broadcast(8),
             )
 
         h_rows = hT.rearrange("(p r) t -> p r t", r=PACK)
-        h_early = keep.tile([P, PACK, J - P], F32, name="h_early")
-        nc.sync.dma_start(h_early[:], h_rows[:, :, 0 : J - P])
-
+        h_first = keep.tile([P, PACK, HALF], F32, name="h_first", tag="h_first", align_bytes=64)
+        h_late = [keep.tile([P, PACK, P], F32, name="h_late%d" % v) for v in range(2)]
         word_table = keep.tile([P, T], I32, name="word_table", align_bytes=64)
+        nc.sync.dma_start(h_first[:], h_rows[:, :, 0:HALF])
         nc.sync.dma_start(word_table[:], x_words[0].rearrange("p c r -> p (c r)").bitcast(I32))
-
-        h_late = keep.tile([P, PACK, P], F32, name="h_late", tag="h_late")
-        nc.sync.dma_start(h_late[:], h_rows[:, :, J - P : J])
+        for v in range(2):
+            nc.sync.dma_start(h_late[v][:], h_rows[:, :, HALF + P * v : HALF + P * (v + 1)])
 
         shift = keep.tile([P, 1], F32, name="shift")
         nc.vector.memset(shift[:], -CAP)
@@ -60,19 +59,27 @@ def tile_picked_zsoft_cap_p_kernel(tc, x_words, x_scales, hT, corr, offs, out):
         nc.scalar.activation(warm[:], shift[:], ACT.Exp)
 
         identity = keep.tile([P, P], F32, name="identity")
-        make_identity(nc, identity[:])
+        zeros = keep.tile([P, P], F32, name="zeros", tag="h_bf", align_bytes=64)
+        nc.gpsimd.memset(zeros[:], 0.0)
+        nc.gpsimd.affine_select(
+            out=identity[:],
+            in_=zeros[:],
+            compare_op=ALU.not_equal,
+            fill=1.0,
+            base=0,
+            pattern=[[-1, P]],
+            channel_multiplier=1,
+        )
 
-        x_codes = keep.tile([P, S], U32, name="x_codes", align_bytes=64)
-        x_plane = keep.tile([P, S], U8, name="x_plane", align_bytes=64)
+        x_plane = keep.tile([P, S], U8, name="x_plane", tag="corr_table", align_bytes=64)
         corr_picked = keep.tile([P, S], F32, name="corr_picked")
-        h_bf = [keep.tile([P, HALF, PACK], BF16, name="h_bf%d" % u, tag="h_bf%d" % u, align_bytes=64) for u in range(2)]
-        h_codes = [keep.tile([P, HALF], U32, name="h_codes%d" % u, align_bytes=64) for u in range(2)]
+        h_bf = keep.tile([P, J, PACK], BF16, name="h_bf", tag="h_bf", align_bytes=64)
+        h_codes = [keep.tile([P, HALF], U32, name="h_codes%d" % u, tag="h_codes%d" % u, align_bytes=64) for u in range(2)]
         h_plane = [keep.tile([P, HALF], U8, name="h_plane%d" % u, align_bytes=64) for u in range(2)]
 
         def interleave(copy, tb, raw):
-            u, v = divmod(tb, 2)
             copy(
-                h_bf[u][:, P * v : P * (v + 1), :].rearrange("p (c i) r -> p c r i", i=4),
+                h_bf[:, P * tb : P * (tb + 1), :].rearrange("p (c i) r -> p c r i", i=4),
                 raw.rearrange("p r (c i) -> p c r i", i=4),
             )
 
@@ -80,7 +87,7 @@ def tile_picked_zsoft_cap_p_kernel(tc, x_words, x_scales, hT, corr, offs, out):
             nc.vector.quantize_mx(
                 out=h_codes[u][:].bitcast(FP8X4),
                 scales=h_plane[u][:],
-                in_=h_bf[u][:].rearrange("p t r -> p (t r)"),
+                in_=h_bf[:, HALF * u : HALF * (u + 1), :].rearrange("p t r -> p (t r)"),
             )
 
         nc.vector.tensor_copy(corr_picked[:], corr_table[:].indirect(offsets[:]))
@@ -88,17 +95,23 @@ def tile_picked_zsoft_cap_p_kernel(tc, x_words, x_scales, hT, corr, offs, out):
         corr_bank = psum.tile([P, 4, P], F32, name="corr_bank", tag="bank7")
         for b in range(4):
             nc.tensor.transpose(corr_bank[:, b, :], corr_picked[:, P * b : P * (b + 1)], identity[:])
-        interleave(nc.scalar.copy, 0, h_early[:, :, 0:P])
-        interleave(nc.vector.tensor_copy, 1, h_early[:, :, P : 2 * P])
-        interleave(nc.scalar.copy, 2, h_early[:, :, 2 * P : 3 * P])
-        quantize(0)
-        half_corr = keep.tile([P, 4], F32, name="half_corr", tag="h_bf0", align_bytes=64)
+        interleave(nc.scalar.copy, 0, h_first[:, :, 0:P])
+        interleave(nc.scalar.copy, 1, h_first[:, :, P : 2 * P])
+        half_corr = keep.tile([P, 4], F32, name="half_corr")
         nc.scalar.mul(half_corr[:], corr_bank[:, :, CORR_ROW], 0.5)
-        interleave(nc.scalar.copy, 3, h_late[:])
-        for b in range(4):
-            nc.vector.tensor_copy(
-                x_codes[:, P * b : P * (b + 1)], word_table[:].bitcast(U32).indirect(offsets[:, 8 * b : 8 * (b + 1)])
-            )
+        x_first = keep.tile([P, P], U32, name="x_first", align_bytes=64)
+        x_rest = keep.tile([P, S - P], U32, name="x_rest", tag="h_first", align_bytes=64)
+        x_codes = [x_first[:]] + [x_rest[:, P * b : P * (b + 1)] for b in range(3)]
+
+        def gather_words(b):
+            nc.vector.tensor_copy(x_codes[b], word_table[:].bitcast(U32).indirect(offsets[:, 8 * b : 8 * (b + 1)]))
+
+        gather_words(0)
+        quantize(0)
+        for b in range(1, 4):
+            gather_words(b)
+        for v in range(2):
+            interleave(nc.scalar.copy, 2 + v, h_late[v][:])
         quantize(1)
 
         capped = {}
@@ -107,14 +120,14 @@ def tile_picked_zsoft_cap_p_kernel(tc, x_words, x_scales, hT, corr, offs, out):
                 bank = psum.tile([P, HALF], F32, name="score", tag="bank%d" % (4 * u + b))
                 nc.tensor.matmul_mx(
                     out=bank[:],
-                    lhsT=x_codes[:, P * b : P * (b + 1)].bitcast(FP8X4),
+                    lhsT=x_codes[b].bitcast(FP8X4),
                     lhsT_scale=x_plane[:, P * b : P * (b + 1)],
                     rhs=h_codes[u][:].bitcast(FP8X4),
                     rhs_scale=h_plane[u][:],
                     start=True,
                     stop=True,
                 )
-                tag = "h_late" if (u, b) == (0, 0) else "capped%d_%d" % (u, b)
+                tag = "capped%d_%d" % (u, b)
                 capped[u, b] = keep.tile([P, HALF], F32, name="capped", tag=tag)
                 nc.scalar.activation(capped[u, b][:], bank[:], ACT.Tanh, bias=half_corr[:, b : b + 1], scale=0.5)
 

@@ -32,25 +32,22 @@ def tile_picked_zsoft_cap_p_kernel(tc, x_words, x_scales, hT, corr, offs, out):
         nc.sync.dma_start(offsets[:], offs)
 
         corr_table = keep.tile([P, T], F32, name="corr_table", tag="corr_table", align_bytes=64)
-        nc.sync.dma_start(corr_table[CORR_ROW:P, :], corr[CORR_ROW:P, :])
-
-        scale_table = keep.tile([P, T], U8, name="scale_table", align_bytes=64)
-        scale_rows = x_scales[0].bitcast(I32)
-        for q in range(4):
-            queue = nc.sync if q == 0 else nc.scalar
-            queue.dma_start(
-                scale_table[32 * q : 32 * (q + 1), :].bitcast(I32),
-                scale_rows[4 * q : 4 * (q + 1), :].partition_broadcast(8),
-            )
+        nc.scalar.dma_start(corr_table[CORR_ROW:P, :], corr[CORR_ROW:P, :])
 
         h_rows = hT.rearrange("(p r) t -> p r t", r=PACK)
         h_first = keep.tile([P, PACK, HALF], F32, name="h_first", tag="h_first", align_bytes=64)
-        h_late = [keep.tile([P, PACK, P], F32, name="h_late%d" % v) for v in range(2)]
-        word_table = keep.tile([P, T], I32, name="word_table", align_bytes=64)
         nc.sync.dma_start(h_first[:], h_rows[:, :, 0:HALF])
+
+        scale_table = keep.tile([P, T], U8, name="scale_table", align_bytes=64)
+        nc.vector.memset(scale_table[:].bitcast(I32), 0)
+        scale_rows = x_scales[0].bitcast(I32)
+        for q in range(4):
+            nc.sync.dma_start(scale_table[32 * q : 32 * q + 4, :].bitcast(I32), scale_rows[4 * q : 4 * (q + 1), :])
+
+        word_table = keep.tile([P, T], I32, name="word_table", align_bytes=64)
         nc.sync.dma_start(word_table[:], x_words[0].rearrange("p c r -> p (c r)").bitcast(I32))
-        for v in range(2):
-            nc.sync.dma_start(h_late[v][:], h_rows[:, :, HALF + P * v : HALF + P * (v + 1)])
+        h_second = keep.tile([P, PACK, HALF], F32, name="h_second")
+        nc.sync.dma_start(h_second[:], h_rows[:, :, HALF:J])
 
         shift = keep.tile([P, 1], F32, name="shift")
         nc.vector.memset(shift[:], -CAP)
@@ -72,22 +69,19 @@ def tile_picked_zsoft_cap_p_kernel(tc, x_words, x_scales, hT, corr, offs, out):
         )
 
         x_plane = keep.tile([P, S], U8, name="x_plane", tag="corr_table", align_bytes=64)
-        corr_picked = keep.tile([P, S], F32, name="corr_picked")
-        h_bf = keep.tile([P, J, PACK], BF16, name="h_bf", tag="h_bf", align_bytes=64)
+        corr_picked = keep.tile([P, S], F32, name="corr_picked", tag="corr_picked", align_bytes=64)
+        bf_first = keep.tile([P, HALF, PACK], BF16, name="bf_first", tag="h_bf", align_bytes=64)
         h_codes = [keep.tile([P, HALF], U32, name="h_codes%d" % u, tag="h_codes%d" % u, align_bytes=64) for u in range(2)]
         h_plane = [keep.tile([P, HALF], U8, name="h_plane%d" % u, align_bytes=64) for u in range(2)]
 
-        def interleave(copy, tb, raw):
-            copy(
-                h_bf[:, P * tb : P * (tb + 1), :].rearrange("p (c i) r -> p c r i", i=4),
-                raw.rearrange("p r (c i) -> p c r i", i=4),
-            )
+        def interleave(copy, grouped, raw):
+            copy(grouped.rearrange("p (c i) r -> p c r i", i=4), raw.rearrange("p r (c i) -> p c r i", i=4))
 
-        def quantize(u):
+        def quantize(u, cols, grouped):
             nc.vector.quantize_mx(
-                out=h_codes[u][:].bitcast(FP8X4),
-                scales=h_plane[u][:],
-                in_=h_bf[:, HALF * u : HALF * (u + 1), :].rearrange("p t r -> p (t r)"),
+                out=h_codes[u][:, cols].bitcast(FP8X4),
+                scales=h_plane[u][:, cols],
+                in_=grouped.rearrange("p t r -> p (t r)"),
             )
 
         nc.vector.tensor_copy(corr_picked[:], corr_table[:].indirect(offsets[:]))
@@ -95,8 +89,8 @@ def tile_picked_zsoft_cap_p_kernel(tc, x_words, x_scales, hT, corr, offs, out):
         corr_bank = psum.tile([P, 4, P], F32, name="corr_bank", tag="bank7")
         for b in range(4):
             nc.tensor.transpose(corr_bank[:, b, :], corr_picked[:, P * b : P * (b + 1)], identity[:])
-        interleave(nc.scalar.copy, 0, h_first[:, :, 0:P])
-        interleave(nc.scalar.copy, 1, h_first[:, :, P : 2 * P])
+        interleave(nc.scalar.copy, bf_first[:, 0:P, :], h_first[:, :, 0:P])
+        interleave(nc.scalar.copy, bf_first[:, P:HALF, :], h_first[:, :, P:HALF])
         half_corr = keep.tile([P, 4], F32, name="half_corr")
         nc.scalar.mul(half_corr[:], corr_bank[:, :, CORR_ROW], 0.5)
         x_first = keep.tile([P, P], U32, name="x_first", align_bytes=64)
@@ -107,12 +101,15 @@ def tile_picked_zsoft_cap_p_kernel(tc, x_words, x_scales, hT, corr, offs, out):
             nc.vector.tensor_copy(x_codes[b], word_table[:].bitcast(U32).indirect(offsets[:, 8 * b : 8 * (b + 1)]))
 
         gather_words(0)
-        quantize(0)
+        quantize(0, slice(0, HALF), bf_first[:])
         for b in range(1, 4):
             gather_words(b)
-        for v in range(2):
-            interleave(nc.scalar.copy, 2 + v, h_late[v][:])
-        quantize(1)
+        bf_third = keep.tile([P, P, PACK], BF16, name="bf_third", tag="corr_picked", align_bytes=64)
+        bf_fourth = keep.tile([P, P, PACK], BF16, name="bf_fourth", tag="h_bf", align_bytes=64)
+        interleave(nc.scalar.copy, bf_third[:], h_second[:, :, 0:P])
+        interleave(nc.vector.tensor_copy, bf_fourth[:], h_second[:, :, P:HALF])
+        quantize(1, slice(0, P), bf_third[:])
+        quantize(1, slice(P, HALF), bf_fourth[:])
 
         capped = {}
         for u in range(2):
@@ -133,7 +130,7 @@ def tile_picked_zsoft_cap_p_kernel(tc, x_words, x_scales, hT, corr, offs, out):
 
         for tb in range(4):
             u, v = divmod(tb, 2)
-            bank = psum.tile([P, S], F32, name="rows", tag="bank%d" % (3 + tb))
+            bank = psum.tile([P, S], F32, name="rows", tag="bank%d" % tb)
             for b in range(4):
                 nc.tensor.transpose(bank[:, P * b : P * (b + 1)], capped[u, b][:, P * v : P * (v + 1)], identity[:])
             weights = keep.tile([P, S], F32, name="weights%d" % tb)
@@ -142,5 +139,13 @@ def tile_picked_zsoft_cap_p_kernel(tc, x_words, x_scales, hT, corr, offs, out):
             result = keep.tile([P, S], F32, name="result%d" % tb)
             nc.scalar.activation(weights[:], bank[:], ACT.Exp, bias=shift[:], scale=CAP, accum_out=total[:])
             nc.vector.reciprocal(inverse[:], total[:])
-            nc.vector.tensor_scalar(result[:], weights[:], inverse[:], None, ALU.mult)
-            nc.sync.dma_start(out[P * tb : P * (tb + 1), :], result[:])
+            rows = out[P * tb : P * (tb + 1), :]
+            if tb < 3:
+                nc.vector.tensor_scalar(result[:], weights[:], inverse[:], None, ALU.mult)
+                nc.sync.dma_start(rows, result[:])
+            else:
+                for c in range(2):
+                    cols = slice(HALF * c, HALF * (c + 1))
+                    nc.vector.tensor_scalar(result[:, cols], weights[:, cols], inverse[:], None, ALU.mult)
+                    queue = nc.sync if c == 0 else nc.scalar
+                    queue.dma_start(rows[:, cols], result[:, cols])

@@ -17,7 +17,13 @@ ALU = mybir.AluOpType
 
 P = 128
 PACK = 4
-HALF = 256
+QUADRANT = 32
+SCALE_ROWS = 4
+LIST_ROWS = 16
+LINE = 4
+HALF = J // 2
+BLOCKS = S // P
+TILES = J // P
 CORR_ROW = P - 1
 CAP = 2.0
 
@@ -28,7 +34,7 @@ def tile_picked_zsoft_cap_p_kernel(tc, x_words, x_scales, hT, corr, offs, out):
         keep = ctx.enter_context(tc.tile_pool(name="keep", bufs=1))
         psum = ctx.enter_context(tc.psum_pool(name="psum", bufs=1))
 
-        offsets = keep.tile([P, S // 16], U16, name="offsets")
+        offsets = keep.tile([P, S // LIST_ROWS], U16, name="offsets")
         nc.sync.dma_start(offsets[:], offs)
 
         corr_table = keep.tile([P, T], F32, name="corr_table", tag="corr_table", align_bytes=64)
@@ -41,8 +47,11 @@ def tile_picked_zsoft_cap_p_kernel(tc, x_words, x_scales, hT, corr, offs, out):
         scale_table = keep.tile([P, T], U8, name="scale_table", align_bytes=64)
         nc.vector.memset(scale_table[:].bitcast(I32), 0)
         scale_rows = x_scales[0].bitcast(I32)
-        for q in range(4):
-            nc.sync.dma_start(scale_table[32 * q : 32 * q + 4, :].bitcast(I32), scale_rows[4 * q : 4 * (q + 1), :])
+        for q in range(P // QUADRANT):
+            nc.sync.dma_start(
+                scale_table[QUADRANT * q : QUADRANT * q + SCALE_ROWS, :].bitcast(I32),
+                scale_rows[SCALE_ROWS * q : SCALE_ROWS * (q + 1), :],
+            )
 
         word_table = keep.tile([P, T], I32, name="word_table", align_bytes=64)
         nc.sync.dma_start(word_table[:], x_words[0].rearrange("p c r -> p (c r)").bitcast(I32))
@@ -52,6 +61,7 @@ def tile_picked_zsoft_cap_p_kernel(tc, x_words, x_scales, hT, corr, offs, out):
         shift = keep.tile([P, 1], F32, name="shift")
         nc.vector.memset(shift[:], -CAP)
         nc.vector.memset(corr_table[0:CORR_ROW, :], 0.0)
+
         warm = keep.tile([P, 1], F32, name="warm")
         nc.scalar.activation(warm[:], shift[:], ACT.Exp)
 
@@ -71,11 +81,11 @@ def tile_picked_zsoft_cap_p_kernel(tc, x_words, x_scales, hT, corr, offs, out):
         x_plane = keep.tile([P, S], U8, name="x_plane", tag="corr_table", align_bytes=64)
         corr_picked = keep.tile([P, S], F32, name="corr_picked", tag="corr_picked", align_bytes=64)
         bf_first = keep.tile([P, HALF, PACK], BF16, name="bf_first", tag="h_bf", align_bytes=64)
-        h_codes = [keep.tile([P, HALF], U32, name="h_codes%d" % u, tag="h_codes%d" % u, align_bytes=64) for u in range(2)]
+        h_codes = [keep.tile([P, HALF], U32, name="h_codes%d" % u, align_bytes=64) for u in range(2)]
         h_plane = [keep.tile([P, HALF], U8, name="h_plane%d" % u, align_bytes=64) for u in range(2)]
 
         def interleave(copy, grouped, raw):
-            copy(grouped.rearrange("p (c i) r -> p c r i", i=4), raw.rearrange("p r (c i) -> p c r i", i=4))
+            copy(grouped.rearrange("p (c i) r -> p c r i", i=LINE), raw.rearrange("p r (c i) -> p c r i", i=LINE))
 
         def quantize(u, cols, grouped):
             nc.vector.quantize_mx(
@@ -86,24 +96,29 @@ def tile_picked_zsoft_cap_p_kernel(tc, x_words, x_scales, hT, corr, offs, out):
 
         nc.vector.tensor_copy(corr_picked[:], corr_table[:].indirect(offsets[:]))
         nc.vector.tensor_copy(x_plane[:], scale_table[:].indirect(offsets[:]))
-        corr_bank = psum.tile([P, 4, P], F32, name="corr_bank", tag="bank7")
-        for b in range(4):
+
+        corr_bank = psum.tile([P, BLOCKS, P], F32, name="corr_bank", tag="bank%d" % (2 * BLOCKS - 1))
+        for b in range(BLOCKS):
             nc.tensor.transpose(corr_bank[:, b, :], corr_picked[:, P * b : P * (b + 1)], identity[:])
         interleave(nc.scalar.copy, bf_first[:, 0:P, :], h_first[:, :, 0:P])
         interleave(nc.scalar.copy, bf_first[:, P:HALF, :], h_first[:, :, P:HALF])
-        half_corr = keep.tile([P, 4], F32, name="half_corr")
-        nc.scalar.mul(half_corr[:], corr_bank[:, :, CORR_ROW], 0.5)
+        half_corr = keep.tile([P, BLOCKS], F32, name="half_corr")
+        nc.scalar.mul(half_corr[:], corr_bank[:, :, CORR_ROW], 1.0 / CAP)
+
         x_first = keep.tile([P, P], U32, name="x_first", align_bytes=64)
         x_rest = keep.tile([P, S - P], U32, name="x_rest", tag="h_first", align_bytes=64)
-        x_codes = [x_first[:]] + [x_rest[:, P * b : P * (b + 1)] for b in range(3)]
+        x_codes = [x_first[:]] + [x_rest[:, P * b : P * (b + 1)] for b in range(BLOCKS - 1)]
+        list_cols = P // LIST_ROWS
 
         def gather_words(b):
-            nc.vector.tensor_copy(x_codes[b], word_table[:].bitcast(U32).indirect(offsets[:, 8 * b : 8 * (b + 1)]))
+            block_offsets = offsets[:, list_cols * b : list_cols * (b + 1)]
+            nc.vector.tensor_copy(x_codes[b], word_table[:].bitcast(U32).indirect(block_offsets))
 
         gather_words(0)
         quantize(0, slice(0, HALF), bf_first[:])
-        for b in range(1, 4):
+        for b in range(1, BLOCKS):
             gather_words(b)
+
         bf_third = keep.tile([P, P, PACK], BF16, name="bf_third", tag="corr_picked", align_bytes=64)
         bf_fourth = keep.tile([P, P, PACK], BF16, name="bf_fourth", tag="h_bf", align_bytes=64)
         interleave(nc.scalar.copy, bf_third[:], h_second[:, :, 0:P])
@@ -113,10 +128,10 @@ def tile_picked_zsoft_cap_p_kernel(tc, x_words, x_scales, hT, corr, offs, out):
 
         capped = {}
         for u in range(2):
-            for b in range(4):
-                bank = psum.tile([P, HALF], F32, name="score", tag="bank%d" % (4 * u + b))
+            for b in range(BLOCKS):
+                score = psum.tile([P, HALF], F32, name="score", tag="bank%d" % (BLOCKS * u + b))
                 nc.tensor.matmul_mx(
-                    out=bank[:],
+                    out=score[:],
                     lhsT=x_codes[b].bitcast(FP8X4),
                     lhsT_scale=x_plane[:, P * b : P * (b + 1)],
                     rhs=h_codes[u][:].bitcast(FP8X4),
@@ -124,28 +139,21 @@ def tile_picked_zsoft_cap_p_kernel(tc, x_words, x_scales, hT, corr, offs, out):
                     start=True,
                     stop=True,
                 )
-                tag = "capped%d_%d" % (u, b)
-                capped[u, b] = keep.tile([P, HALF], F32, name="capped", tag=tag)
-                nc.scalar.activation(capped[u, b][:], bank[:], ACT.Tanh, bias=half_corr[:, b : b + 1], scale=0.5)
+                capped[u, b] = keep.tile([P, HALF], F32, name="capped", tag="capped%d_%d" % (u, b))
+                nc.scalar.activation(
+                    capped[u, b][:], score[:], ACT.Tanh, bias=half_corr[:, b : b + 1], scale=1.0 / CAP
+                )
 
-        for tb in range(4):
+        for tb in range(TILES):
             u, v = divmod(tb, 2)
-            bank = psum.tile([P, S], F32, name="rows", tag="bank%d" % tb)
-            for b in range(4):
-                nc.tensor.transpose(bank[:, P * b : P * (b + 1)], capped[u, b][:, P * v : P * (v + 1)], identity[:])
+            turned = psum.tile([P, S], F32, name="rows", tag="bank%d" % tb)
+            for b in range(BLOCKS):
+                nc.tensor.transpose(turned[:, P * b : P * (b + 1)], capped[u, b][:, P * v : P * (v + 1)], identity[:])
             weights = keep.tile([P, S], F32, name="weights%d" % tb)
             total = keep.tile([P, 1], F32, name="total%d" % tb)
             inverse = keep.tile([P, 1], F32, name="inverse%d" % tb)
             result = keep.tile([P, S], F32, name="result%d" % tb)
-            nc.scalar.activation(weights[:], bank[:], ACT.Exp, bias=shift[:], scale=CAP, accum_out=total[:])
+            nc.scalar.activation(weights[:], turned[:], ACT.Exp, bias=shift[:], scale=CAP, accum_out=total[:])
             nc.vector.reciprocal(inverse[:], total[:])
-            rows = out[P * tb : P * (tb + 1), :]
-            if tb < 3:
-                nc.vector.tensor_scalar(result[:], weights[:], inverse[:], None, ALU.mult)
-                nc.sync.dma_start(rows, result[:])
-            else:
-                for c in range(2):
-                    cols = slice(HALF * c, HALF * (c + 1))
-                    nc.vector.tensor_scalar(result[:, cols], weights[:, cols], inverse[:], None, ALU.mult)
-                    queue = nc.sync if c == 0 else nc.scalar
-                    queue.dma_start(rows[:, cols], result[:, cols])
+            nc.vector.tensor_scalar(result[:], weights[:], inverse[:], None, ALU.mult)
+            nc.sync.dma_start(out[P * tb : P * (tb + 1), :], result[:])

@@ -25,6 +25,7 @@ HALF = J // 2
 BLOCKS = S // P
 TILES = J // P
 CORR_ROW = P - 1
+LAST_SHARE = 160
 CAP = 2.0
 
 
@@ -153,7 +154,10 @@ def tile_picked_zsoft_cap_p_kernel(tc, x_words, x_scales, hT, corr, offs, out):
             total = keep.tile([P, 1], F32, name="total%d" % tb)
             inverse = keep.tile([P, 1], F32, name="inverse%d" % tb)
             result = keep.tile([P, S], F32, name="result%d" % tb)
-            nc.scalar.activation(weights[:], turned[:], ACT.Exp, bias=shift[:], scale=CAP, accum_out=total[:])
+            nc.scalar.activation(weights[:], turned[:], ACT.Exp, bias=-CAP, scale=CAP, accum_out=total[:])
             nc.vector.reciprocal(inverse[:], total[:])
-            nc.vector.tensor_scalar(result[:], weights[:], inverse[:], None, ALU.mult)
+            cut = S - LAST_SHARE if tb == TILES - 1 else S
+            nc.vector.tensor_scalar(result[:, 0:cut], weights[:, 0:cut], inverse[:], None, ALU.mult)
+            if cut < S:
+                nc.scalar.activation(result[:, cut:S], weights[:, cut:S], ACT.Copy, scale=inverse[:])
             nc.sync.dma_start(out[P * tb : P * (tb + 1), :], result[:])

@@ -38,7 +38,7 @@ def tile_picked_zsoft_cap_p_kernel(tc, x_words, x_scales, hT, corr, offs, out):
         offsets = keep.tile([P, S // LIST_ROWS], U16, name="offsets")
         nc.sync.dma_start(offsets[:], offs)
 
-        corr_table = keep.tile([P, T], F32, name="corr_table", tag="corr_table", align_bytes=64)
+        corr_table = keep.tile([P, T], F32, name="corr_table", align_bytes=64)
         nc.scalar.dma_start(corr_table[CORR_ROW:P, :], corr[CORR_ROW:P, :])
 
         h_rows = hT.rearrange("(p r) t -> p r t", r=PACK)
@@ -79,7 +79,7 @@ def tile_picked_zsoft_cap_p_kernel(tc, x_words, x_scales, hT, corr, offs, out):
             channel_multiplier=1,
         )
 
-        x_plane = keep.tile([P, S], U8, name="x_plane", tag="corr_table", align_bytes=64)
+        x_plane = keep.tile([P, S], U8, name="x_plane", align_bytes=64)
         corr_picked = keep.tile([P, S], F32, name="corr_picked", tag="corr_picked", align_bytes=64)
         bf_first = keep.tile([P, HALF, PACK], BF16, name="bf_first", tag="h_bf", align_bytes=64)
         h_codes = [keep.tile([P, HALF], U32, name="h_codes%d" % u, align_bytes=64) for u in range(2)]
@@ -123,31 +123,32 @@ def tile_picked_zsoft_cap_p_kernel(tc, x_words, x_scales, hT, corr, offs, out):
         bf_third = keep.tile([P, P, PACK], BF16, name="bf_third", tag="corr_picked", align_bytes=64)
         bf_fourth = keep.tile([P, P, PACK], BF16, name="bf_fourth", tag="h_bf", align_bytes=64)
         interleave(nc.scalar.copy, bf_third[:], h_second[:, :, 0:P])
-        interleave(nc.vector.tensor_copy, bf_fourth[:], h_second[:, :, P:HALF])
         quantize(1, slice(0, P), bf_third[:])
+        interleave(nc.vector.tensor_copy, bf_fourth[:], h_second[:, :, P:HALF])
         quantize(1, slice(P, HALF), bf_fourth[:])
 
         capped = {}
-        for u in range(2):
+        for g, (u, cols) in enumerate(((0, slice(0, HALF)), (1, slice(0, P)), (1, slice(P, HALF)))):
+            width = cols.stop - cols.start
             for b in range(BLOCKS):
-                score = psum.tile([P, HALF], F32, name="score", tag="bank%d" % (BLOCKS * u + b))
+                score = psum.tile([P, width], F32, name="score", tag="bank%d" % (BLOCKS * (g % 2) + b))
                 nc.tensor.matmul_mx(
                     out=score[:],
                     lhsT=x_codes[b].bitcast(FP8X4),
                     lhsT_scale=x_plane[:, P * b : P * (b + 1)],
-                    rhs=h_codes[u][:].bitcast(FP8X4),
-                    rhs_scale=h_plane[u][:],
+                    rhs=h_codes[u][:, cols].bitcast(FP8X4),
+                    rhs_scale=h_plane[u][:, cols],
                     start=True,
                     stop=True,
                 )
-                capped[u, b] = keep.tile([P, HALF], F32, name="capped", tag="capped%d_%d" % (u, b))
+                capped[g, b] = keep.tile([P, width], F32, name="capped", tag="capped%d_%d" % (g, b))
                 nc.scalar.activation(
-                    capped[u, b][:], score[:], ACT.Tanh, bias=half_corr[:, b : b + 1], scale=1.0 / CAP
+                    capped[g, b][:], score[:], ACT.Tanh, bias=half_corr[:, b : b + 1], scale=1.0 / CAP
                 )
 
         for tb in range(TILES):
-            u, v = divmod(tb, 2)
-            turned = psum.tile([P, S], F32, name="rows", tag="bank%d" % tb)
+            u, v = max(tb - 1, 0), int(tb == 1)
+            turned = psum.tile([P, S], F32, name="rows", tag="bank%d" % (BLOCKS + tb))
             for b in range(BLOCKS):
                 nc.tensor.transpose(turned[:, P * b : P * (b + 1)], capped[u, b][:, P * v : P * (v + 1)], identity[:])
             weights = keep.tile([P, S], F32, name="weights%d" % tb)

@@ -155,7 +155,7 @@ def tile_picked_zsoft_cap_p_kernel(tc, x_words, x_scales, hT, corr, offs, out):
             total = keep.tile([P, 1], F32, name="total%d" % tb)
             inverse = keep.tile([P, 1], F32, name="inverse%d" % tb)
             result = keep.tile([P, S], F32, name="result%d" % tb)
-            nc.scalar.activation(weights[:], turned[:], ACT.Exp, bias=-CAP, scale=CAP, accum_out=total[:])
+            nc.scalar.activation(weights[:], turned[:], ACT.Exp, bias=shift[:], scale=CAP, accum_out=total[:])
             nc.vector.reciprocal(inverse[:], total[:])
             cut = S - LAST_SHARE if tb == TILES - 1 else S
             nc.vector.tensor_scalar(result[:, 0:cut], weights[:, 0:cut], inverse[:], None, ALU.mult)

@@ -95,7 +95,11 @@ def tile_picked_zsoft_cap_p_kernel(tc, x_words, x_scales, hT, corr, offs, out):
                 in_=grouped.rearrange("p t r -> p (t r)"),
             )
 
-        nc.vector.tensor_copy(corr_picked[:], corr_table[:].indirect(offsets[:]))
+        half_list = HALF // LIST_ROWS
+        nc.vector.tensor_copy(corr_picked[:, 0:HALF], corr_table[:].indirect(offsets[:, 0:half_list]))
+        nc.scalar.activation(
+            corr_picked[:, HALF:S], corr_table[:].indirect(offsets[:, half_list : 2 * half_list]), ACT.Copy
+        )
         nc.vector.tensor_copy(x_plane[:], scale_table[:].indirect(offsets[:]))
 
         corr_bank = psum.tile([P, BLOCKS, P], F32, name="corr_bank", tag="bank%d" % (2 * BLOCKS - 1))

@@ -48,10 +48,10 @@ def tile_picked_zsoft_cap_p_kernel(tc, x_words, x_scales, hT, corr, offs, out):
         scale_table = keep.tile([P, T], U8, name="scale_table", align_bytes=64)
         nc.vector.memset(scale_table[:].bitcast(I32), 0)
         scale_rows = x_scales[0].bitcast(I32)
-        for q in range(P // QUADRANT):
+        for i in range(SCALE_ROWS):
             nc.sync.dma_start(
-                scale_table[QUADRANT * q : QUADRANT * q + SCALE_ROWS, :].bitcast(I32),
-                scale_rows[SCALE_ROWS * q : SCALE_ROWS * (q + 1), :],
+                scale_table[i:P:QUADRANT, :].bitcast(I32),
+                scale_rows[i : K // QUADRANT : SCALE_ROWS, :],
             )
 
         word_table = keep.tile([P, T], I32, name="word_table", align_bytes=64)

@@ -26,6 +26,7 @@ BLOCKS = S // P
 TILES = J // P
 CORR_ROW = P - 1
 LAST_SHARE = 160
+FIRST_SHARE = 128
 CAP = 2.0
 
 
@@ -33,6 +34,7 @@ def tile_picked_zsoft_cap_p_kernel(tc, x_words, x_scales, hT, corr, offs, out):
     nc = tc.nc
     with ExitStack() as ctx:
         keep = ctx.enter_context(tc.tile_pool(name="keep", bufs=1))
+        held = ctx.enter_context(tc.tile_pool(name="held", bufs=1))
         psum = ctx.enter_context(tc.psum_pool(name="psum", bufs=1))
 
         offsets = keep.tile([P, S // LIST_ROWS], U16, name="offsets")
@@ -43,7 +45,7 @@ def tile_picked_zsoft_cap_p_kernel(tc, x_words, x_scales, hT, corr, offs, out):
 
         h_rows = hT.rearrange("(p r) t -> p r t", r=PACK)
         h_first = keep.tile([P, PACK, HALF], F32, name="h_first", tag="h_first", align_bytes=64)
-        nc.sync.dma_start(h_first[:], h_rows[:, :, 0:HALF])
+        nc.sync.dma_start(h_first[:, 0 : PACK // 2, :], h_rows[:, 0 : PACK // 2, 0:HALF])
 
         scale_table = keep.tile([P, T], U8, name="scale_table", align_bytes=64)
         nc.vector.memset(scale_table[:].bitcast(I32), 0)
@@ -54,10 +56,13 @@ def tile_picked_zsoft_cap_p_kernel(tc, x_words, x_scales, hT, corr, offs, out):
                 scale_rows[i : K // QUADRANT : SCALE_ROWS, :],
             )
 
+        nc.sync.dma_start(h_first[:, PACK // 2 : PACK, :], h_rows[:, PACK // 2 : PACK, 0:HALF])
         word_table = keep.tile([P, T], I32, name="word_table", align_bytes=64)
         nc.sync.dma_start(word_table[:], x_words[0].rearrange("p c r -> p (c r)").bitcast(I32))
-        h_second = keep.tile([P, PACK, HALF], F32, name="h_second")
-        nc.sync.dma_start(h_second[:], h_rows[:, :, HALF:J])
+        h_third = keep.tile([P, PACK, P], F32, name="h_third", tag="h_third", align_bytes=64)
+        nc.sync.dma_start(h_third[:], h_rows[:, :, HALF : HALF + P])
+        h_fourth = keep.tile([P, PACK, P], F32, name="h_fourth")
+        nc.sync.dma_start(h_fourth[:], h_rows[:, :, HALF + P : J])
 
         shift = keep.tile([P, 1], F32, name="shift")
         nc.vector.memset(shift[:], -CAP)
@@ -67,7 +72,7 @@ def tile_picked_zsoft_cap_p_kernel(tc, x_words, x_scales, hT, corr, offs, out):
         nc.scalar.activation(warm[:], shift[:], ACT.Exp)
 
         identity = keep.tile([P, P], F32, name="identity")
-        zeros = keep.tile([P, P], F32, name="zeros", tag="h_bf", align_bytes=64)
+        zeros = held.tile([P, P], F32, name="zeros", offset=2 * PACK * HALF - 2 * P, align_bytes=64)
         nc.gpsimd.memset(zeros[:], 0.0)
         nc.gpsimd.affine_select(
             out=identity[:],
@@ -79,9 +84,11 @@ def tile_picked_zsoft_cap_p_kernel(tc, x_words, x_scales, hT, corr, offs, out):
             channel_multiplier=1,
         )
 
-        x_plane = keep.tile([P, S], U8, name="x_plane", align_bytes=64)
+        plane_early = keep.tile([P, S - P], U8, name="plane_early", align_bytes=64)
+        plane_late = held.tile([P, P], U8, name="plane_late", offset=2 * PACK * HALF, align_bytes=64)
+        x_plane = [plane_early[:, P * b : P * (b + 1)] for b in range(BLOCKS - 1)] + [plane_late[:]]
         corr_picked = keep.tile([P, S], F32, name="corr_picked", tag="corr_picked", align_bytes=64)
-        bf_first = keep.tile([P, HALF, PACK], BF16, name="bf_first", tag="h_bf", align_bytes=64)
+        bf_first = held.tile([P, HALF, PACK], BF16, name="bf_first", offset=0, align_bytes=64)
         h_codes = [keep.tile([P, HALF], U32, name="h_codes%d" % u, align_bytes=64) for u in range(2)]
         h_plane = [keep.tile([P, HALF], U8, name="h_plane%d" % u, align_bytes=64) for u in range(2)]
 
@@ -95,40 +102,36 @@ def tile_picked_zsoft_cap_p_kernel(tc, x_words, x_scales, hT, corr, offs, out):
                 in_=grouped.rearrange("p t r -> p (t r)"),
             )
 
-        half_list = HALF // LIST_ROWS
-        nc.vector.tensor_copy(corr_picked[:, 0:HALF], corr_table[:].indirect(offsets[:, 0:half_list]))
-        nc.scalar.activation(
-            corr_picked[:, HALF:S], corr_table[:].indirect(offsets[:, half_list : 2 * half_list]), ACT.Copy
-        )
-        nc.vector.tensor_copy(x_plane[:], scale_table[:].indirect(offsets[:]))
+        nc.scalar.activation(corr_picked[:], corr_table[:].indirect(offsets[:]), ACT.Copy)
+        list_cols = P // LIST_ROWS
+        early_cols = list_cols * (BLOCKS - 1)
+        nc.vector.tensor_copy(plane_early[:], scale_table[:].indirect(offsets[:, 0:early_cols]))
 
         corr_bank = psum.tile([P, BLOCKS, P], F32, name="corr_bank", tag="bank%d" % (2 * BLOCKS - 1))
         for b in range(BLOCKS):
             nc.tensor.transpose(corr_bank[:, b, :], corr_picked[:, P * b : P * (b + 1)], identity[:])
-        interleave(nc.scalar.copy, bf_first[:, 0:P, :], h_first[:, :, 0:P])
-        interleave(nc.scalar.copy, bf_first[:, P:HALF, :], h_first[:, :, P:HALF])
+        interleave(nc.scalar.copy, bf_first[:, 0:FIRST_SHARE, :], h_first[:, :, 0:FIRST_SHARE])
+        interleave(nc.vector.tensor_copy, bf_first[:, FIRST_SHARE:HALF, :], h_first[:, :, FIRST_SHARE:HALF])
+        nc.vector.tensor_copy(plane_late[:], scale_table[:].indirect(offsets[:, early_cols : early_cols + list_cols]))
         half_corr = keep.tile([P, BLOCKS], F32, name="half_corr")
         nc.scalar.mul(half_corr[:], corr_bank[:, :, CORR_ROW], 1.0 / CAP)
 
-        x_first = keep.tile([P, P], U32, name="x_first", align_bytes=64)
-        x_rest = keep.tile([P, S - P], U32, name="x_rest", tag="h_first", align_bytes=64)
-        x_codes = [x_first[:]] + [x_rest[:, P * b : P * (b + 1)] for b in range(BLOCKS - 1)]
-        list_cols = P // LIST_ROWS
+        x_all = keep.tile([P, S], U32, name="x_all", tag="h_first", align_bytes=64)
+        x_codes = [x_all[:, P * b : P * (b + 1)] for b in range(BLOCKS)]
 
         def gather_words(b):
             block_offsets = offsets[:, list_cols * b : list_cols * (b + 1)]
             nc.vector.tensor_copy(x_codes[b], word_table[:].bitcast(U32).indirect(block_offsets))
 
-        gather_words(0)
         quantize(0, slice(0, HALF), bf_first[:])
-        for b in range(1, BLOCKS):
+        for b in range(BLOCKS):
             gather_words(b)
 
         bf_third = keep.tile([P, P, PACK], BF16, name="bf_third", tag="corr_picked", align_bytes=64)
-        bf_fourth = keep.tile([P, P, PACK], BF16, name="bf_fourth", tag="h_bf", align_bytes=64)
-        interleave(nc.scalar.copy, bf_third[:], h_second[:, :, 0:P])
+        bf_fourth = keep.tile([P, P, PACK], BF16, name="bf_fourth", tag="h_third", align_bytes=64)
+        interleave(nc.scalar.copy, bf_third[:], h_third[:])
         quantize(1, slice(0, P), bf_third[:])
-        interleave(nc.vector.tensor_copy, bf_fourth[:], h_second[:, :, P:HALF])
+        interleave(nc.vector.tensor_copy, bf_fourth[:], h_fourth[:])
         quantize(1, slice(P, HALF), bf_fourth[:])
 
         capped = {}
@@ -139,7 +142,7 @@ def tile_picked_zsoft_cap_p_kernel(tc, x_words, x_scales, hT, corr, offs, out):
                 nc.tensor.matmul_mx(
                     out=score[:],
                     lhsT=x_codes[b].bitcast(FP8X4),
-                    lhsT_scale=x_plane[:, P * b : P * (b + 1)],
+                    lhsT_scale=x_plane[b],
                     rhs=h_codes[u][:, cols].bitcast(FP8X4),
                     rhs_scale=h_plane[u][:, cols],
                     start=True,

@@ -72,11 +72,11 @@ def tile_picked_zsoft_cap_p_kernel(tc, x_words, x_scales, hT, corr, offs, out):
         nc.scalar.activation(warm[:], shift[:], ACT.Exp)
 
         identity = keep.tile([P, P], F32, name="identity")
-        zeros = held.tile([P, P], F32, name="zeros", offset=2 * PACK * HALF - 2 * P, align_bytes=64)
-        nc.gpsimd.memset(zeros[:], 0.0)
+        zeros = held.tile([P, 2 * P], F32, name="zeros", offset=2 * PACK * HALF - 2 * P, align_bytes=64)
+        nc.gpsimd.memset(zeros[:, 0:P], 0.0)
         nc.gpsimd.affine_select(
             out=identity[:],
-            in_=zeros[:],
+            in_=zeros[:, 0:P],
             compare_op=ALU.not_equal,
             fill=1.0,
             base=0,
@@ -87,7 +87,7 @@ def tile_picked_zsoft_cap_p_kernel(tc, x_words, x_scales, hT, corr, offs, out):
         plane_early = keep.tile([P, S - P], U8, name="plane_early", align_bytes=64)
         plane_late = held.tile([P, P], U8, name="plane_late", offset=2 * PACK * HALF, align_bytes=64)
         x_plane = [plane_early[:, P * b : P * (b + 1)] for b in range(BLOCKS - 1)] + [plane_late[:]]
-        corr_picked = keep.tile([P, S], F32, name="corr_picked", tag="corr_picked", align_bytes=64)
+        corr_early = keep.tile([P, S - P], F32, name="corr_early", align_bytes=64)
         bf_first = held.tile([P, HALF, PACK], BF16, name="bf_first", offset=0, align_bytes=64)
         h_codes = [keep.tile([P, HALF], U32, name="h_codes%d" % u, align_bytes=64) for u in range(2)]
         h_plane = [keep.tile([P, HALF], U8, name="h_plane%d" % u, align_bytes=64) for u in range(2)]
@@ -102,15 +102,19 @@ def tile_picked_zsoft_cap_p_kernel(tc, x_words, x_scales, hT, corr, offs, out):
                 in_=grouped.rearrange("p t r -> p (t r)"),
             )
 
-        nc.scalar.activation(corr_picked[:], corr_table[:].indirect(offsets[:]), ACT.Copy)
         list_cols = P // LIST_ROWS
         early_cols = list_cols * (BLOCKS - 1)
+        nc.scalar.activation(corr_early[:], corr_table[:].indirect(offsets[:, 0:early_cols]), ACT.Copy)
         nc.vector.tensor_copy(plane_early[:], scale_table[:].indirect(offsets[:, 0:early_cols]))
 
         corr_bank = psum.tile([P, BLOCKS, P], F32, name="corr_bank", tag="bank%d" % (2 * BLOCKS - 1))
-        for b in range(BLOCKS):
-            nc.tensor.transpose(corr_bank[:, b, :], corr_picked[:, P * b : P * (b + 1)], identity[:])
+        for b in range(BLOCKS - 1):
+            nc.tensor.transpose(corr_bank[:, b, :], corr_early[:, P * b : P * (b + 1)], identity[:])
         interleave(nc.scalar.copy, bf_first[:, 0:FIRST_SHARE, :], h_first[:, :, 0:FIRST_SHARE])
+        corr_late = held.tile([P, P], F32, name="corr_late", offset=2 * PACK * HALF + 2 * P, align_bytes=64)
+        late_offsets = offsets[:, early_cols : early_cols + list_cols]
+        nc.scalar.activation(corr_late[:], corr_table[:].indirect(late_offsets), ACT.Copy)
+        nc.tensor.transpose(corr_bank[:, BLOCKS - 1, :], corr_late[:], identity[:])
         interleave(nc.vector.tensor_copy, bf_first[:, FIRST_SHARE:HALF, :], h_first[:, :, FIRST_SHARE:HALF])
         nc.vector.tensor_copy(plane_late[:], scale_table[:].indirect(offsets[:, early_cols : early_cols + list_cols]))
         half_corr = keep.tile([P, BLOCKS], F32, name="half_corr")
@@ -127,7 +131,7 @@ def tile_picked_zsoft_cap_p_kernel(tc, x_words, x_scales, hT, corr, offs, out):
         for b in range(BLOCKS):
             gather_words(b)
 
-        bf_third = keep.tile([P, P, PACK], BF16, name="bf_third", tag="corr_picked", align_bytes=64)
+        bf_third = held.tile([P, P, PACK], BF16, name="bf_third", offset=2 * PACK * HALF + 2 * P, align_bytes=64)
         bf_fourth = keep.tile([P, P, PACK], BF16, name="bf_fourth", tag="h_third", align_bytes=64)
         interleave(nc.scalar.copy, bf_third[:], h_third[:])
         quantize(1, slice(0, P), bf_third[:])

@@ -66,14 +66,14 @@ def tile_picked_zsoft_cap_p_kernel(tc, x_words, x_scales, hT, corr, offs, out):
 
         shift = keep.tile([P, 1], F32, name="shift")
         nc.vector.memset(shift[:], -CAP)
+        zeros = held.tile([P, 2 * P], F32, name="zeros", offset=2 * PACK * HALF - 2 * P, align_bytes=64)
+        nc.vector.memset(zeros[:, 0:P], 0.0)
         nc.vector.memset(corr_table[0:CORR_ROW, :], 0.0)
 
         warm = keep.tile([P, 1], F32, name="warm")
         nc.scalar.activation(warm[:], shift[:], ACT.Exp)
 
         identity = keep.tile([P, P], F32, name="identity")
-        zeros = held.tile([P, 2 * P], F32, name="zeros", offset=2 * PACK * HALF - 2 * P, align_bytes=64)
-        nc.gpsimd.memset(zeros[:, 0:P], 0.0)
         nc.gpsimd.affine_select(
             out=identity[:],
             in_=zeros[:, 0:P],

@@ -50,11 +50,15 @@ def tile_picked_zsoft_cap_p_kernel(tc, x_words, x_scales, hT, corr, offs, out):
         scale_table = keep.tile([P, T], U8, name="scale_table", align_bytes=64)
         nc.vector.memset(scale_table[:].bitcast(I32), 0)
         scale_rows = x_scales[0].bitcast(I32)
-        for i in range(SCALE_ROWS):
-            nc.sync.dma_start(
+
+        def load_scale_row(queue, i):
+            queue.dma_start(
                 scale_table[i:P:QUADRANT, :].bitcast(I32),
                 scale_rows[i : K // QUADRANT : SCALE_ROWS, :],
             )
+
+        for i in range(SCALE_ROWS - 1):
+            load_scale_row(nc.sync, i)
 
         nc.sync.dma_start(h_first[:, PACK // 2 : PACK, :], h_rows[:, PACK // 2 : PACK, 0:HALF])
         word_table = keep.tile([P, T], I32, name="word_table", align_bytes=64)
@@ -72,6 +76,7 @@ def tile_picked_zsoft_cap_p_kernel(tc, x_words, x_scales, hT, corr, offs, out):
 
         warm = keep.tile([P, 1], F32, name="warm")
         nc.scalar.activation(warm[:], shift[:], ACT.Exp)
+        load_scale_row(nc.scalar, SCALE_ROWS - 1)
 
         identity = keep.tile([P, P], F32, name="identity")
         nc.gpsimd.affine_select(
@@ -104,7 +109,13 @@ def tile_picked_zsoft_cap_p_kernel(tc, x_words, x_scales, hT, corr, offs, out):
 
         list_cols = P // LIST_ROWS
         early_cols = list_cols * (BLOCKS - 1)
-        nc.scalar.activation(corr_early[:], corr_table[:].indirect(offsets[:, 0:early_cols]), ACT.Copy)
+        shared = BLOCKS - 2
+        nc.scalar.activation(
+            corr_early[:, 0 : P * shared], corr_table[:].indirect(offsets[:, 0 : list_cols * shared]), ACT.Copy
+        )
+        nc.vector.tensor_copy(
+            corr_early[:, P * shared : S - P], corr_table[:].indirect(offsets[:, list_cols * shared : early_cols])
+        )
         nc.vector.tensor_copy(plane_early[:], scale_table[:].indirect(offsets[:, 0:early_cols]))
 
         corr_bank = psum.tile([P, BLOCKS, P], F32, name="corr_bank", tag="bank%d" % (2 * BLOCKS - 1))

from contextlib import ExitStack

import concourse.mybir as mybir

K, T, S, J = 512, 1024, 512, 512
FLOPS = 2 * K * S * J

F32 = mybir.dt.float32
BF16 = mybir.dt.bfloat16
I32 = mybir.dt.int32
U32 = mybir.dt.uint32
U16 = mybir.dt.uint16
U8 = mybir.dt.uint8
FP8X4 = mybir.dt.float8_e4m3fn_x4
ACT = mybir.ActivationFunctionType
ALU = mybir.AluOpType

P = 128
PACK = 4
QUADRANT = 32
SCALE_ROWS = 4
LIST_ROWS = 16
LINE = 4
HALF = J // 2
BLOCKS = S // P
TILES = J // P
CORR_ROW = P - 1
LAST_SHARE = 160
FIRST_SHARE = 128
CAP = 2.0


def tile_picked_zsoft_cap_p_kernel(tc, x_words, x_scales, hT, corr, offs, out):
    nc = tc.nc
    with ExitStack() as ctx:
        keep = ctx.enter_context(tc.tile_pool(name="keep", bufs=1))
        held = ctx.enter_context(tc.tile_pool(name="held", bufs=1))
        psum = ctx.enter_context(tc.psum_pool(name="psum", bufs=1))

        offsets = keep.tile([P, S // LIST_ROWS], U16, name="offsets")
        nc.sync.dma_start(offsets[:], offs)

        corr_table = keep.tile([P, T], F32, name="corr_table", align_bytes=64)
        nc.scalar.dma_start(corr_table[CORR_ROW:P, :], corr[CORR_ROW:P, :])

        h_rows = hT.rearrange("(p r) t -> p r t", r=PACK)
        h_first = keep.tile([P, PACK, HALF], F32, name="h_first", tag="h_first", align_bytes=64)
        nc.sync.dma_start(h_first[:, 0 : PACK // 2, :], h_rows[:, 0 : PACK // 2, 0:HALF])

        scale_table = keep.tile([P, T], U8, name="scale_table", align_bytes=64)
        nc.vector.memset(scale_table[:].bitcast(I32), 0)
        scale_rows = x_scales[0].bitcast(I32)

        def load_scale_row(queue, i):
            queue.dma_start(
                scale_table[i:P:QUADRANT, :].bitcast(I32),
                scale_rows[i : K // QUADRANT : SCALE_ROWS, :],
            )

        for i in range(SCALE_ROWS - 1):
            load_scale_row(nc.sync, i)

        nc.sync.dma_start(h_first[:, PACK // 2 : PACK, :], h_rows[:, PACK // 2 : PACK, 0:HALF])
        word_table = keep.tile([P, T], I32, name="word_table", align_bytes=64)
        nc.sync.dma_start(word_table[:], x_words[0].rearrange("p c r -> p (c r)").bitcast(I32))
        h_third = keep.tile([P, PACK, P], F32, name="h_third", tag="h_third", align_bytes=64)
        nc.sync.dma_start(h_third[:], h_rows[:, :, HALF : HALF + P])
        h_fourth = keep.tile([P, PACK, P], F32, name="h_fourth")
        nc.sync.dma_start(h_fourth[:], h_rows[:, :, HALF + P : J])

        shift = keep.tile([P, 1], F32, name="shift")
        nc.vector.memset(shift[:], -CAP)
        zeros = held.tile([P, 2 * P], F32, name="zeros", offset=2 * PACK * HALF - 2 * P, align_bytes=64)
        nc.vector.memset(zeros[:, 0:P], 0.0)
        nc.vector.memset(corr_table[0:CORR_ROW, :], 0.0)

        warm = keep.tile([P, 1], F32, name="warm")
        nc.scalar.activation(warm[:], shift[:], ACT.Exp)
        load_scale_row(nc.scalar, SCALE_ROWS - 1)

        identity = keep.tile([P, P], F32, name="identity")
        nc.gpsimd.affine_select(
            out=identity[:],
            in_=zeros[:, 0:P],
            compare_op=ALU.not_equal,
            fill=1.0,
            base=0,
            pattern=[[-1, P]],
            channel_multiplier=1,
        )

        plane_early = keep.tile([P, S - P], U8, name="plane_early", align_bytes=64)
        plane_late = held.tile([P, P], U8, name="plane_late", offset=2 * PACK * HALF, align_bytes=64)
        x_plane = [plane_early[:, P * b : P * (b + 1)] for b in range(BLOCKS - 1)] + [plane_late[:]]
        corr_early = keep.tile([P, S - P], F32, name="corr_early", align_bytes=64)
        bf_first = held.tile([P, HALF, PACK], BF16, name="bf_first", offset=0, align_bytes=64)
        h_codes = [keep.tile([P, HALF], U32, name="h_codes%d" % u, align_bytes=64) for u in range(2)]
        h_plane = [keep.tile([P, HALF], U8, name="h_plane%d" % u, align_bytes=64) for u in range(2)]

        def interleave(copy, grouped, raw):
            copy(grouped.rearrange("p (c i) r -> p c r i", i=LINE), raw.rearrange("p r (c i) -> p c r i", i=LINE))

        def quantize(u, cols, grouped):
            nc.vector.quantize_mx(
                out=h_codes[u][:, cols].bitcast(FP8X4),
                scales=h_plane[u][:, cols],
                in_=grouped.rearrange("p t r -> p (t r)"),
            )

        list_cols = P // LIST_ROWS
        early_cols = list_cols * (BLOCKS - 1)
        shared = BLOCKS - 2
        nc.scalar.activation(
            corr_early[:, 0 : P * shared], corr_table[:].indirect(offsets[:, 0 : list_cols * shared]), ACT.Copy
        )
        nc.vector.tensor_copy(
            corr_early[:, P * shared : S - P], corr_table[:].indirect(offsets[:, list_cols * shared : early_cols])
        )
        nc.vector.tensor_copy(plane_early[:], scale_table[:].indirect(offsets[:, 0:early_cols]))

        corr_bank = psum.tile([P, BLOCKS, P], F32, name="corr_bank", tag="bank%d" % (2 * BLOCKS - 1))
        for b in range(BLOCKS - 1):
            nc.tensor.transpose(corr_bank[:, b, :], corr_early[:, P * b : P * (b + 1)], identity[:])
        interleave(nc.scalar.copy, bf_first[:, 0:FIRST_SHARE, :], h_first[:, :, 0:FIRST_SHARE])
        corr_late = held.tile([P, P], F32, name="corr_late", offset=2 * PACK * HALF + 2 * P, align_bytes=64)
        late_offsets = offsets[:, early_cols : early_cols + list_cols]
        nc.scalar.activation(corr_late[:], corr_table[:].indirect(late_offsets), ACT.Copy)
        nc.tensor.transpose(corr_bank[:, BLOCKS - 1, :], corr_late[:], identity[:])
        interleave(nc.vector.tensor_copy, bf_first[:, FIRST_SHARE:HALF, :], h_first[:, :, FIRST_SHARE:HALF])
        nc.vector.tensor_copy(plane_late[:], scale_table[:].indirect(offsets[:, early_cols : early_cols + list_cols]))
        half_corr = keep.tile([P, BLOCKS], F32, name="half_corr")
        nc.scalar.mul(half_corr[:], corr_bank[:, :, CORR_ROW], 1.0 / CAP)

        x_all = keep.tile([P, S], U32, name="x_all", tag="h_first", align_bytes=64)
        x_codes = [x_all[:, P * b : P * (b + 1)] for b in range(BLOCKS)]

        def gather_words(b):
            block_offsets = offsets[:, list_cols * b : list_cols * (b + 1)]
            nc.vector.tensor_copy(x_codes[b], word_table[:].bitcast(U32).indirect(block_offsets))

        quantize(0, slice(0, HALF), bf_first[:])
        for b in range(BLOCKS):
            gather_words(b)

        bf_third = held.tile([P, P, PACK], BF16, name="bf_third", offset=2 * PACK * HALF + 2 * P, align_bytes=64)
        bf_fourth = keep.tile([P, P, PACK], BF16, name="bf_fourth", tag="h_third", align_bytes=64)
        interleave(nc.scalar.copy, bf_third[:], h_third[:])
        quantize(1, slice(0, P), bf_third[:])
        interleave(nc.vector.tensor_copy, bf_fourth[:], h_fourth[:])
        quantize(1, slice(P, HALF), bf_fourth[:])

        capped = {}
        for g, (u, cols) in enumerate(((0, slice(0, HALF)), (1, slice(0, P)), (1, slice(P, HALF)))):
            width = cols.stop - cols.start
            for b in range(BLOCKS):
                score = psum.tile([P, width], F32, name="score", tag="bank%d" % (BLOCKS * (g % 2) + b))
                nc.tensor.matmul_mx(
                    out=score[:],
                    lhsT=x_codes[b].bitcast(FP8X4),
                    lhsT_scale=x_plane[b],
                    rhs=h_codes[u][:, cols].bitcast(FP8X4),
                    rhs_scale=h_plane[u][:, cols],
                    start=True,
                    stop=True,
                )
                capped[g, b] = keep.tile([P, width], F32, name="capped", tag="capped%d_%d" % (g, b))
                nc.scalar.activation(
                    capped[g, b][:], score[:], ACT.Tanh, bias=half_corr[:, b : b + 1], scale=1.0 / CAP
                )

        for tb in range(TILES):
            u, v = max(tb - 1, 0), int(tb == 1)
            turned = psum.tile([P, S], F32, name="rows", tag="bank%d" % (BLOCKS + tb))
            for b in range(BLOCKS):
                nc.tensor.transpose(turned[:, P * b : P * (b + 1)], capped[u, b][:, P * v : P * (v + 1)], identity[:])
            weights = keep.tile([P, S], F32, name="weights%d" % tb)
            total = keep.tile([P, 1], F32, name="total%d" % tb)
            inverse = keep.tile([P, 1], F32, name="inverse%d" % tb)
            result = keep.tile([P, S], F32, name="result%d" % tb)
            nc.scalar.activation(weights[:], turned[:], ACT.Exp, bias=shift[:], scale=CAP, accum_out=total[:])
            nc.vector.reciprocal(inverse[:], total[:])
            cut = S - LAST_SHARE if tb == TILES - 1 else S
            nc.vector.tensor_scalar(result[:, 0:cut], weights[:, 0:cut], inverse[:], None, ALU.mult)
            if cut < S:
                nc.scalar.activation(result[:, cut:S], weights[:, cut:S], ACT.Copy, scale=inverse[:])
            nc.sync.dma_start(out[P * tb : P * (tb + 1), :], result[:])
